import numpy as np
import ml_dtypes


def mxq(x, axis, fmt="e4m3"):
    dtype, down = {"e4m3": (ml_dtypes.float8_e4m3fn, 7), "e5m2": (ml_dtypes.float8_e5m2, 14)}[fmt]
    v = np.moveaxis(np.asarray(x, np.float32).astype(ml_dtypes.bfloat16).astype(np.float64), axis, -1)
    blocks = v.reshape(v.shape[:-1] + (-1, 32))
    amax = np.abs(blocks).max(-1, keepdims=True)
    byte = np.maximum(np.where(amax > 0, np.frexp(amax)[1] - 1 + 127, 0) - down, 1)
    scale = np.exp2(byte - 127.0)
    codes = (blocks / scale).astype(np.float32).astype(dtype).astype(np.float64)
    return np.moveaxis((codes * scale).reshape(v.shape), -1, axis)


WIDE = False


def mx_kscale(k):
    if not WIDE:
        return np.ones(k)
    levels = np.array([30, -30])
    if k % 512:
        return np.exp2(np.random.permutation(np.resize(levels, k // 32))).repeat(32)
    a = np.empty((k // 512, 16))
    for p in range(k // 512):
        a[p, :8] = np.random.permutation(np.resize(levels, 8))
        for g in range(8):
            far = levels[np.abs(levels - a[p, g]) >= 10]
            a[p, g + 8] = far[np.random.randint(len(far))]
    return np.exp2(a.ravel()).repeat(32)


def f64(x):
    return np.asarray(x).astype(np.float64)


def striped(idx):
    return np.tile(np.asarray(idx).reshape(-1, 16).T, (8, 1)).astype(np.uint16)


def unstriped(offs):
    return offs[:16].T.reshape(-1).astype(np.int64)


T, K, R, J = 1024, 512, 2048, 512


def setup_inputs():
    n = np.random.standard_normal
    idx = np.random.permutation(R)[:J]
    ft = mx_kscale(T)
    return {
        "xt": (n((T, K)) * ft[:, None]).astype(np.float32),
        "gh": (n((T, R)) * np.exp(0.5 * n((T, 1))) / ft[:, None]).astype(np.float32),
        "mom": (1.0 * n((K, R))).astype(np.float32),
        "lr": (np.random.uniform(0.01, 0.05, (K, 1))).astype(np.float32),
        "offs": striped(idx),
    }


def reference(xt, gh, mom, lr, offs):
    idx = unstriped(offs)
    xtq = mxq(f64(xt), 0, "e4m3")
    ghidxq = mxq(f64(gh)[:, idx], 0, "e5m2")
    w = xtq.T @ ghidxq
    y = 0.9 * f64(mom)[:, idx] - f64(lr) * w
    return y

@@ -1,0 +1,122 @@
+from contextlib import ExitStack
+
+import concourse.mybir as mybir
+
+T, K, R, J = 1024, 512, 2048, 512
+FLOPS = 2 * T * K * J
+
+F32 = mybir.dt.float32
+BF16 = mybir.dt.bfloat16
+U32 = mybir.dt.uint32
+U16 = mybir.dt.uint16
+U8 = mybir.dt.uint8
+E4M3 = mybir.dt.float8_e4m3fn_x4
+E5M2 = mybir.dt.float8_e5m2_x4
+MULT = mybir.AluOpType.mult
+SUB = mybir.AluOpType.subtract
+COPY = mybir.ActivationFunctionType.Copy
+
+P = 128
+PACK = 4
+T_PASS = P * PACK
+PASSES = T // T_PASS
+BLOCKS = K // P
+LIST_ROWS = 16
+MOMENTUM = 0.9
+
+
+def tile_list_hot_neuron_wgrad_kernel(tc, xt, gh, mom, lr, offs, out):
+    nc = tc.nc
+    gh_rows = gh.rearrange("(a p i) r -> a i p r", a=PASSES, i=PACK)
+    xt_rows = xt.rearrange("(a p i) k -> a p i k", a=PASSES, i=PACK)
+    mom_rows = mom.rearrange("(p c) r -> c p r", c=BLOCKS)
+    out_rows = out.rearrange("(p c) j -> c p j", c=BLOCKS)
+    lr_rows = lr.rearrange("(p c) o -> p (c o)", c=BLOCKS)
+
+    with ExitStack() as ctx:
+        keep = ctx.enter_context(tc.tile_pool(name="keep", bufs=1))
+        psum = ctx.enter_context(tc.psum_pool(name="psum", bufs=1))
+
+        offsets = keep.tile([P, J // LIST_ROWS], U16, name="offsets")
+        steps = keep.tile([P, BLOCKS], F32, name="steps")
+        gh_raw = [[keep.tile([P, R], F32, name=f"gh_raw{a}_{i}") for i in range(PACK)] for a in range(PASSES)]
+        xt_raw = [keep.tile([P, PACK, K], F32, name=f"xt_raw{a}") for a in range(PASSES)]
+        mom_raw = [keep.tile([P, R], F32, name=f"mom_raw{c}") for c in range(BLOCKS)]
+
+        nc.sync.dma_start(out=gh_raw[0][0][:], in_=gh_rows[0, 0])
+        nc.sync.dma_start(offsets[:], offs)
+        nc.sync.dma_start(out=steps[:], in_=lr_rows)
+        for i in range(1, PACK):
+            nc.sync.dma_start(out=gh_raw[0][i][:], in_=gh_rows[0, i])
+        for a in range(PASSES):
+            nc.sync.dma_start(out=xt_raw[a][:], in_=xt_rows[a])
+        for i in range(PACK):
+            nc.sync.dma_start(out=gh_raw[1][i][:], in_=gh_rows[1, i])
+        for c in range(BLOCKS):
+            nc.sync.dma_start(out=mom_raw[c][:], in_=mom_rows[c])
+
+        acc = [psum.tile([P, J], F32, name=f"acc{c}") for c in range(BLOCKS)]
+        gh_codes = [keep.tile([P, J], U32, name=f"gh_codes{a}", align_bytes=64) for a in range(PASSES)]
+        gh_scales = [keep.tile([P, J], U8, name=f"gh_scales{a}", align_bytes=64) for a in range(PASSES)]
+        xt_codes = [keep.tile([P, K], U32, name=f"xt_codes{a}", align_bytes=64) for a in range(PASSES)]
+        xt_scales = [keep.tile([P, K], U8, name=f"xt_scales{a}", align_bytes=64) for a in range(PASSES)]
+
+        def quantize_gh(a):
+            woven = keep.tile([P, J, PACK], BF16, name=f"gh_woven{a}", align_bytes=64)
+            for i in range(PACK):
+                nc.vector.tensor_copy(out=woven[:, :, i], in_=gh_raw[a][i][:].indirect(offsets[:]))
+            nc.vector.quantize_mx(
+                out=gh_codes[a][:].bitcast(E5M2),
+                scales=gh_scales[a][:],
+                in_=woven[:].rearrange("p j i -> p (j i)"),
+            )
+
+        def quantize_xt(a):
+            woven = keep.tile([P, BLOCKS, P, PACK], BF16, name=f"xt_woven{a}", align_bytes=64)
+            nc.scalar.activation(
+                out=woven[:].rearrange("p c m i -> p m i c"),
+                in_=xt_raw[a][:].rearrange("p i (m c) -> p m i c", c=BLOCKS),
+                func=COPY,
+            )
+            nc.vector.quantize_mx(
+                out=xt_codes[a][:].bitcast(E4M3),
+                scales=xt_scales[a][:],
+                in_=woven[:].rearrange("p c m i -> p (c m i)"),
+            )
+
+        def multiply(a):
+            for c in range(BLOCKS):
+                cols = slice(c * P, (c + 1) * P)
+                nc.tensor.matmul_mx(
+                    out=acc[c][:],
+                    lhsT=xt_codes[a][:, cols].bitcast(E4M3),
+                    lhsT_scale=xt_scales[a][:, cols],
+                    rhs=gh_codes[a][:].bitcast(E5M2),
+                    rhs_scale=gh_scales[a][:],
+                    start=(a == 0),
+                    stop=(a == PASSES - 1),
+                )
+
+        quantize_gh(0)
+        quantize_xt(0)
+        multiply(0)
+        quantize_xt(1)
+        quantize_gh(1)
+        multiply(1)
+
+        for c in range(BLOCKS):
+            update = keep.tile([P, J], F32, name=f"update{c}")
+            nc.scalar.activation(out=update[:], in_=acc[c][:], func=COPY, scale=steps[:, c : c + 1])
+            pieces = 2 if c == BLOCKS - 1 else 1
+            width = J // pieces
+            picked = [keep.tile([P, width], F32, name=f"picked{c}_{h}") for h in range(pieces)]
+            for h in range(pieces):
+                entries = offsets[:, h * width // LIST_ROWS : (h + 1) * width // LIST_ROWS]
+                nc.vector.tensor_copy(out=picked[h][:], in_=mom_raw[c][:].indirect(entries))
+            for h in range(pieces):
+                cols = slice(h * width, (h + 1) * width)
+                result = keep.tile([P, width], F32, name=f"result{c}_{h}")
+                nc.vector.scalar_tensor_tensor(
+                    out=result[:], in0=picked[h][:], scalar=MOMENTUM, in1=update[:, cols], op0=MULT, op1=SUB
+                )
+                nc.sync.dma_start(out=out_rows[c, :, cols], in_=result[:])

@@ -13,7 +13,7 @@ U8 = mybir.dt.uint8
 E4M3 = mybir.dt.float8_e4m3fn_x4
 E5M2 = mybir.dt.float8_e5m2_x4
 MULT = mybir.AluOpType.mult
-SUB = mybir.AluOpType.subtract
+ADD = mybir.AluOpType.add
 COPY = mybir.ActivationFunctionType.Copy
 
 P = 128
@@ -23,11 +23,13 @@ PASSES = T // T_PASS
 BLOCKS = K // P
 LIST_ROWS = 16
 MOMENTUM = 0.9
+GH_LOADS = [[4], [2, 1, 1]]
+LAST_PIECES = [320, 192]
 
 
 def tile_list_hot_neuron_wgrad_kernel(tc, xt, gh, mom, lr, offs, out):
     nc = tc.nc
-    gh_rows = gh.rearrange("(a p i) r -> a i p r", a=PASSES, i=PACK)
+    gh_rows = gh.rearrange("(a p i) r -> a p i r", a=PASSES, i=PACK)
     xt_rows = xt.rearrange("(a p i) k -> a p i k", a=PASSES, i=PACK)
     mom_rows = mom.rearrange("(p c) r -> c p r", c=BLOCKS)
     out_rows = out.rearrange("(p c) j -> c p j", c=BLOCKS)
@@ -39,19 +41,24 @@ def tile_list_hot_neuron_wgrad_kernel(tc, xt, gh, mom, lr, offs, out):
 
         offsets = keep.tile([P, J // LIST_ROWS], U16, name="offsets")
         steps = keep.tile([P, BLOCKS], F32, name="steps")
-        gh_raw = [[keep.tile([P, R], F32, name=f"gh_raw{a}_{i}") for i in range(PACK)] for a in range(PASSES)]
         xt_raw = [keep.tile([P, PACK, K], F32, name=f"xt_raw{a}") for a in range(PASSES)]
         mom_raw = [keep.tile([P, R], F32, name=f"mom_raw{c}") for c in range(BLOCKS)]
 
-        nc.sync.dma_start(out=gh_raw[0][0][:], in_=gh_rows[0, 0])
+        def load_gh(a):
+            planes = []
+            for count in GH_LOADS[a]:
+                first = len(planes)
+                raw = keep.tile([P, count * R], F32, name=f"gh_raw{a}_{first}")
+                nc.sync.dma_start(out=raw[:], in_=gh_rows[a, :, first : first + count, :].rearrange("p i r -> p (i r)"))
+                planes.extend(raw[:, n * R : (n + 1) * R] for n in range(count))
+            return planes
+
+        gh_planes = [load_gh(0)]
         nc.sync.dma_start(offsets[:], offs)
         nc.sync.dma_start(out=steps[:], in_=lr_rows)
-        for i in range(1, PACK):
-            nc.sync.dma_start(out=gh_raw[0][i][:], in_=gh_rows[0, i])
         for a in range(PASSES):
             nc.sync.dma_start(out=xt_raw[a][:], in_=xt_rows[a])
-        for i in range(PACK):
-            nc.sync.dma_start(out=gh_raw[1][i][:], in_=gh_rows[1, i])
+        gh_planes.append(load_gh(1))
         for c in range(BLOCKS):
             nc.sync.dma_start(out=mom_raw[c][:], in_=mom_rows[c])
 
@@ -64,7 +71,7 @@ def tile_list_hot_neuron_wgrad_kernel(tc, xt, gh, mom, lr, offs, out):
         def quantize_gh(a):
             woven = keep.tile([P, J, PACK], BF16, name=f"gh_woven{a}", align_bytes=64)
             for i in range(PACK):
-                nc.vector.tensor_copy(out=woven[:, :, i], in_=gh_raw[a][i][:].indirect(offsets[:]))
+                nc.vector.tensor_copy(out=woven[:, :, i], in_=gh_planes[a][i].indirect(offsets[:]))
             nc.vector.quantize_mx(
                 out=gh_codes[a][:].bitcast(E5M2),
                 scales=gh_scales[a][:],
@@ -97,6 +104,9 @@ def tile_list_hot_neuron_wgrad_kernel(tc, xt, gh, mom, lr, offs, out):
                     stop=(a == PASSES - 1),
                 )
 
+        factors = keep.tile([P, BLOCKS], F32, name="factors")
+        nc.scalar.activation(out=factors[:], in_=steps[:], func=COPY, scale=-1.0 / MOMENTUM)
+
         quantize_gh(0)
         quantize_xt(0)
         multiply(0)
@@ -104,19 +114,18 @@ def tile_list_hot_neuron_wgrad_kernel(tc, xt, gh, mom, lr, offs, out):
         quantize_gh(1)
         multiply(1)
 
+        updates = [keep.tile([P, J], F32, name=f"update{c}") for c in range(BLOCKS)]
         for c in range(BLOCKS):
-            update = keep.tile([P, J], F32, name=f"update{c}")
-            nc.scalar.activation(out=update[:], in_=acc[c][:], func=COPY, scale=steps[:, c : c + 1])
-            pieces = 2 if c == BLOCKS - 1 else 1
-            width = J // pieces
-            picked = [keep.tile([P, width], F32, name=f"picked{c}_{h}") for h in range(pieces)]
-            for h in range(pieces):
-                entries = offsets[:, h * width // LIST_ROWS : (h + 1) * width // LIST_ROWS]
-                nc.vector.tensor_copy(out=picked[h][:], in_=mom_raw[c][:].indirect(entries))
-            for h in range(pieces):
-                cols = slice(h * width, (h + 1) * width)
-                result = keep.tile([P, width], F32, name=f"result{c}_{h}")
-                nc.vector.scalar_tensor_tensor(
-                    out=result[:], in0=picked[h][:], scalar=MOMENTUM, in1=update[:, cols], op0=MULT, op1=SUB
-                )
+            nc.scalar.activation(out=updates[c][:], in_=acc[c][:], func=COPY, scale=factors[:, c : c + 1])
+
+        for c in range(BLOCKS):
+            first = 0
+            for width in LAST_PIECES if c == BLOCKS - 1 else [J]:
+                cols = slice(first, first + width)
+                entries = offsets[:, first // LIST_ROWS : (first + width) // LIST_ROWS]
+                mixed = keep.tile([P, width], F32, name=f"mixed{c}_{first}")
+                result = keep.tile([P, width], F32, name=f"result{c}_{first}")
+                nc.vector.tensor_tensor(out=mixed[:], in0=mom_raw[c][:].indirect(entries), in1=updates[c][:, cols], op=ADD)
+                nc.scalar.activation(out=result[:], in_=mixed[:], func=COPY, scale=MOMENTUM)
                 nc.sync.dma_start(out=out_rows[c, :, cols], in_=result[:])
+                first += width

@@ -23,7 +23,6 @@ PASSES = T // T_PASS
 BLOCKS = K // P
 LIST_ROWS = 16
 MOMENTUM = 0.9
-GH_LOADS = [[4], [2, 1, 1]]
 LAST_PIECES = [320, 192]
 
 
@@ -44,21 +43,20 @@ def tile_list_hot_neuron_wgrad_kernel(tc, xt, gh, mom, lr, offs, out):
         xt_raw = [keep.tile([P, PACK, K], F32, name=f"xt_raw{a}") for a in range(PASSES)]
         mom_raw = [keep.tile([P, R], F32, name=f"mom_raw{c}") for c in range(BLOCKS)]
 
-        def load_gh(a):
-            planes = []
-            for count in GH_LOADS[a]:
-                first = len(planes)
-                raw = keep.tile([P, count * R], F32, name=f"gh_raw{a}_{first}")
-                nc.sync.dma_start(out=raw[:], in_=gh_rows[a, :, first : first + count, :].rearrange("p i r -> p (i r)"))
-                planes.extend(raw[:, n * R : (n + 1) * R] for n in range(count))
-            return planes
+        def load_gh(a, first, count):
+            raw = keep.tile([P, count * R], F32, name=f"gh_raw{a}_{first}")
+            nc.sync.dma_start(out=raw[:], in_=gh_rows[a, :, first : first + count, :].rearrange("p i r -> p (i r)"))
+            return [raw[:, n * R : (n + 1) * R] for n in range(count)]
 
-        gh_planes = [load_gh(0)]
+        gh_planes = [load_gh(0, 0, 2), []]
         nc.sync.dma_start(offsets[:], offs)
         nc.sync.dma_start(out=steps[:], in_=lr_rows)
+        gh_planes[0].extend(load_gh(0, 2, 2))
+        gh_planes[1].extend(load_gh(1, 0, 2))
         for a in range(PASSES):
             nc.sync.dma_start(out=xt_raw[a][:], in_=xt_rows[a])
-        gh_planes.append(load_gh(1))
+        gh_planes[1].extend(load_gh(1, 2, 1))
+        gh_planes[1].extend(load_gh(1, 3, 1))
         for c in range(BLOCKS):
             nc.sync.dma_start(out=mom_raw[c][:], in_=mom_rows[c])
 
@@ -125,7 +123,13 @@ def tile_list_hot_neuron_wgrad_kernel(tc, xt, gh, mom, lr, offs, out):
                 entries = offsets[:, first // LIST_ROWS : (first + width) // LIST_ROWS]
                 mixed = keep.tile([P, width], F32, name=f"mixed{c}_{first}")
                 result = keep.tile([P, width], F32, name=f"result{c}_{first}")
-                nc.vector.tensor_tensor(out=mixed[:], in0=mom_raw[c][:].indirect(entries), in1=updates[c][:, cols], op=ADD)
+                if c == 0:
+                    picked = keep.tile([P, J], F32, name="picked")
+                    nc.vector.tensor_copy(out=picked[:], in_=mom_raw[c][:].indirect(entries))
+                    momentum = picked[:]
+                else:
+                    momentum = mom_raw[c][:].indirect(entries)
+                nc.vector.tensor_tensor(out=mixed[:], in0=momentum, in1=updates[c][:, cols], op=ADD)
                 nc.scalar.activation(out=result[:], in_=mixed[:], func=COPY, scale=MOMENTUM)
                 nc.sync.dma_start(out=out_rows[c, :, cols], in_=result[:])
                 first += width

@@ -23,13 +23,13 @@ PASSES = T // T_PASS
 BLOCKS = K // P
 LIST_ROWS = 16
 MOMENTUM = 0.9
-LAST_PIECES = [320, 192]
+LAST_PIECES = [256, 160, 96]
 
 
 def tile_list_hot_neuron_wgrad_kernel(tc, xt, gh, mom, lr, offs, out):
     nc = tc.nc
     gh_rows = gh.rearrange("(a p i) r -> a p i r", a=PASSES, i=PACK)
-    xt_rows = xt.rearrange("(a p i) k -> a p i k", a=PASSES, i=PACK)
+    xt_rows = xt.rearrange("(a p i) k -> p a (i k)", a=PASSES, i=PACK)
     mom_rows = mom.rearrange("(p c) r -> c p r", c=BLOCKS)
     out_rows = out.rearrange("(p c) j -> c p j", c=BLOCKS)
     lr_rows = lr.rearrange("(p c) o -> p (c o)", c=BLOCKS)
@@ -40,7 +40,7 @@ def tile_list_hot_neuron_wgrad_kernel(tc, xt, gh, mom, lr, offs, out):
 
         offsets = keep.tile([P, J // LIST_ROWS], U16, name="offsets")
         steps = keep.tile([P, BLOCKS], F32, name="steps")
-        xt_raw = [keep.tile([P, PACK, K], F32, name=f"xt_raw{a}") for a in range(PASSES)]
+        xt_raw = keep.tile([P, PASSES, PACK * K], F32, name="xt_raw")
         mom_raw = [keep.tile([P, R], F32, name=f"mom_raw{c}") for c in range(BLOCKS)]
 
         def load_gh(a, first, count):
@@ -53,8 +53,7 @@ def tile_list_hot_neuron_wgrad_kernel(tc, xt, gh, mom, lr, offs, out):
         nc.sync.dma_start(out=steps[:], in_=lr_rows)
         gh_planes[0].extend(load_gh(0, 2, 2))
         gh_planes[1].extend(load_gh(1, 0, 2))
-        for a in range(PASSES):
-            nc.sync.dma_start(out=xt_raw[a][:], in_=xt_rows[a])
+        nc.sync.dma_start(out=xt_raw[:], in_=xt_rows)
         gh_planes[1].extend(load_gh(1, 2, 1))
         gh_planes[1].extend(load_gh(1, 3, 1))
         for c in range(BLOCKS):
@@ -78,11 +77,12 @@ def tile_list_hot_neuron_wgrad_kernel(tc, xt, gh, mom, lr, offs, out):
 
         def quantize_xt(a):
             woven = keep.tile([P, BLOCKS, P, PACK], BF16, name=f"xt_woven{a}", align_bytes=64)
-            nc.scalar.activation(
-                out=woven[:].rearrange("p c m i -> p m i c"),
-                in_=xt_raw[a][:].rearrange("p i (m c) -> p m i c", c=BLOCKS),
-                func=COPY,
-            )
+            target = woven[:].rearrange("p c m i -> p m i c")
+            source = xt_raw[:, a, :].rearrange("p (i m c) -> p m i c", i=PACK, c=BLOCKS)
+            if a == 0:
+                nc.vector.tensor_copy(out=target, in_=source)
+            else:
+                nc.scalar.activation(out=target, in_=source, func=COPY)
             nc.vector.quantize_mx(
                 out=xt_codes[a][:].bitcast(E4M3),
                 scales=xt_scales[a][:],

from contextlib import ExitStack

import concourse.mybir as mybir

T, K, R, J = 1024, 512, 2048, 512
FLOPS = 2 * T * K * J

F32 = mybir.dt.float32
BF16 = mybir.dt.bfloat16
U32 = mybir.dt.uint32
U16 = mybir.dt.uint16
U8 = mybir.dt.uint8
E4M3 = mybir.dt.float8_e4m3fn_x4
E5M2 = mybir.dt.float8_e5m2_x4
MULT = mybir.AluOpType.mult
ADD = mybir.AluOpType.add
COPY = mybir.ActivationFunctionType.Copy

P = 128
PACK = 4
T_PASS = P * PACK
PASSES = T // T_PASS
BLOCKS = K // P
LIST_ROWS = 16
MOMENTUM = 0.9
LAST_PIECES = [256, 160, 96]


def tile_list_hot_neuron_wgrad_kernel(tc, xt, gh, mom, lr, offs, out):
    nc = tc.nc
    gh_rows = gh.rearrange("(a p i) r -> a p i r", a=PASSES, i=PACK)
    xt_rows = xt.rearrange("(a p i) k -> p a (i k)", a=PASSES, i=PACK)
    mom_rows = mom.rearrange("(p c) r -> c p r", c=BLOCKS)
    out_rows = out.rearrange("(p c) j -> c p j", c=BLOCKS)
    lr_rows = lr.rearrange("(p c) o -> p (c o)", c=BLOCKS)

    with ExitStack() as ctx:
        keep = ctx.enter_context(tc.tile_pool(name="keep", bufs=1))
        psum = ctx.enter_context(tc.psum_pool(name="psum", bufs=1))

        offsets = keep.tile([P, J // LIST_ROWS], U16, name="offsets")
        steps = keep.tile([P, BLOCKS], F32, name="steps")
        xt_raw = keep.tile([P, PASSES, PACK * K], F32, name="xt_raw")
        mom_raw = [keep.tile([P, R], F32, name=f"mom_raw{c}") for c in range(BLOCKS)]

        def load_gh(a, first, count):
            raw = keep.tile([P, count * R], F32, name=f"gh_raw{a}_{first}")
            nc.sync.dma_start(out=raw[:], in_=gh_rows[a, :, first : first + count, :].rearrange("p i r -> p (i r)"))
            return [raw[:, n * R : (n + 1) * R] for n in range(count)]

        gh_planes = [load_gh(0, 0, 2), []]
        nc.sync.dma_start(offsets[:], offs)
        nc.sync.dma_start(out=steps[:], in_=lr_rows)
        gh_planes[0].extend(load_gh(0, 2, 2))
        gh_planes[1].extend(load_gh(1, 0, 2))
        nc.sync.dma_start(out=xt_raw[:], in_=xt_rows)
        gh_planes[1].extend(load_gh(1, 2, 1))
        gh_planes[1].extend(load_gh(1, 3, 1))
        for c in range(BLOCKS):
            nc.sync.dma_start(out=mom_raw[c][:], in_=mom_rows[c])

        acc = [psum.tile([P, J], F32, name=f"acc{c}") for c in range(BLOCKS)]
        gh_codes = [keep.tile([P, J], U32, name=f"gh_codes{a}", align_bytes=64) for a in range(PASSES)]
        gh_scales = [keep.tile([P, J], U8, name=f"gh_scales{a}", align_bytes=64) for a in range(PASSES)]
        xt_codes = [keep.tile([P, K], U32, name=f"xt_codes{a}", align_bytes=64) for a in range(PASSES)]
        xt_scales = [keep.tile([P, K], U8, name=f"xt_scales{a}", align_bytes=64) for a in range(PASSES)]

        def quantize_gh(a):
            woven = keep.tile([P, J, PACK], BF16, name=f"gh_woven{a}", align_bytes=64)
            for i in range(PACK):
                nc.vector.tensor_copy(out=woven[:, :, i], in_=gh_planes[a][i].indirect(offsets[:]))
            nc.vector.quantize_mx(
                out=gh_codes[a][:].bitcast(E5M2),
                scales=gh_scales[a][:],
                in_=woven[:].rearrange("p j i -> p (j i)"),
            )

        def quantize_xt(a):
            woven = keep.tile([P, BLOCKS, P, PACK], BF16, name=f"xt_woven{a}", align_bytes=64)
            target = woven[:].rearrange("p c m i -> p m i c")
            source = xt_raw[:, a, :].rearrange("p (i m c) -> p m i c", i=PACK, c=BLOCKS)
            if a == 0:
                nc.vector.tensor_copy(out=target, in_=source)
            else:
                nc.scalar.activation(out=target, in_=source, func=COPY)
            nc.vector.quantize_mx(
                out=xt_codes[a][:].bitcast(E4M3),
                scales=xt_scales[a][:],
                in_=woven[:].rearrange("p c m i -> p (c m i)"),
            )

        def multiply(a):
            for c in range(BLOCKS):
                cols = slice(c * P, (c + 1) * P)
                nc.tensor.matmul_mx(
                    out=acc[c][:],
                    lhsT=xt_codes[a][:, cols].bitcast(E4M3),
                    lhsT_scale=xt_scales[a][:, cols],
                    rhs=gh_codes[a][:].bitcast(E5M2),
                    rhs_scale=gh_scales[a][:],
                    start=(a == 0),
                    stop=(a == PASSES - 1),
                )

        factors = keep.tile([P, BLOCKS], F32, name="factors")
        nc.scalar.activation(out=factors[:], in_=steps[:], func=COPY, scale=-1.0 / MOMENTUM)

        quantize_gh(0)
        quantize_xt(0)
        multiply(0)
        quantize_xt(1)
        quantize_gh(1)
        multiply(1)

        updates = [keep.tile([P, J], F32, name=f"update{c}") for c in range(BLOCKS)]
        for c in range(BLOCKS):
            nc.scalar.activation(out=updates[c][:], in_=acc[c][:], func=COPY, scale=factors[:, c : c + 1])

        for c in range(BLOCKS):
            first = 0
            for width in LAST_PIECES if c == BLOCKS - 1 else [J]:
                cols = slice(first, first + width)
                entries = offsets[:, first // LIST_ROWS : (first + width) // LIST_ROWS]
                mixed = keep.tile([P, width], F32, name=f"mixed{c}_{first}")
                result = keep.tile([P, width], F32, name=f"result{c}_{first}")
                if c == 0:
                    picked = keep.tile([P, J], F32, name="picked")
                    nc.vector.tensor_copy(out=picked[:], in_=mom_raw[c][:].indirect(entries))
                    momentum = picked[:]
                else:
                    momentum = mom_raw[c][:].indirect(entries)
                nc.vector.tensor_tensor(out=mixed[:], in0=momentum, in1=updates[c][:, cols], op=ADD)
                nc.scalar.activation(out=result[:], in_=mixed[:], func=COPY, scale=MOMENTUM)
                nc.sync.dma_start(out=out_rows[c, :, cols], in_=result[:])
                first += width
